import numpy as np
CORES = [0,1,2,3,4,5,6,7,8,9,10,11,12,13,14,15,16,17,18,19,20,21,22,23,24,25,26,27,28,29,30,31,32,33,34,35,36,37,38,39,40,41,42,43,44,45,46,47,48,49,50,51,52,53,54,55,56,57,58,59,60,61,62,63,64,65,66,67,68,69,70,71,72,73,74,75,76,77,78,79,80,81,82,83,84,85,86,87,88,89,90,91,92,93,94,95,96,97,98,99,100,101,102,103,104,105,106,107,108,109,110,111,112,113,114,115,116,117,118,119,120,121,122,123,124,125,126,127,128,129,130,131,132,133,134,135,136,137,138,139,140,141,142,143,144,145,146,147,148,149,150,151,152,153,154,155,156,157,158,159,160,161,162,163,164,165,166,167,168,169,170,171,172,173,174,175,176,177,178,179,180,181,182,183,184,185,186,187,188,189,190,191,192,193,194,195,196,197,198,199,200,201,202,203,204,205,206,207,208,209,210,211,212,213,214,215,216,217,218,219,220,221,222,223,224,225,226,227,228,229,230,231,232,233,234,235,236,237,238,239,240,241,242,243,244,245,246,247,248,249,250,251,252,253,254,255]
N = 256
def setup_inputs(rng):
    return {"x": rng.standard_normal((N, 128, 16), dtype=np.float32)}
def reference(x):
    g = np.concatenate(list(x), axis=1)
    return {"y": np.broadcast_to(g, (N,) + g.shape)}

@@ -1,0 +1,96 @@
+import concourse.bass as bass
+
+BLK = 16
+CHIPBLK = 8 * BLK
+RANGE = 4 * CHIPBLK
+
+SCRATCH = {
+    "land": ("sbuf", [128, 256 * BLK], "float32"),
+    "xs": ("sbuf", [128, BLK], "float32"),
+}
+SEMAPHORES = ["loaded", "stored", "sent", "hop1", "hop2", "hop3", "hop4"]
+
+
+def owner_of(chip, blk):
+    return 4 * (blk // 16) + ((blk % 16) // 4 - chip // 4) % 4
+
+
+def collector_of(chip, blk):
+    o = owner_of(chip, blk)
+    return o if o % 4 >= 2 else o + 2
+
+
+def rank_program(g, core, T, topo):
+    host, chip, k = topo.host(core), topo.chip(core), core % 8
+    pos = k % 4
+    land, sem = T.land, T.sem
+    sent = 0
+
+    def world(h, c, i):
+        return 128 * h + 8 * c + i
+
+    def here(i):
+        return world(host, chip, i)
+
+    def cols(blk, n=1):
+        return land[:, CHIPBLK * blk:CHIPBLK * (blk + n)]
+
+    def transfer(src, out, dests, mask, remote_sem):
+        ids = []
+        for d in dests:
+            rid, pid = topo.addr(d, core)
+            ids.append(bass.DstId(rid=rid, pnc=pid))
+        return bass.RemoteDMATransfer(dst_ids=ids, dma_engine_mask=mask, remote_sem=remote_sem,
+                                      srcs=[src], dsts=[out for d in dests])
+
+    rank = T.rank_of(core)
+    mine = land[:, BLK * rank:BLK * (rank + 1)]
+    gatherer = 4 * host
+    staged = mine if k == gatherer else T.xs[:]
+    g.dma_start(staged, T.x[:]).then_inc(sem.loaded, 16)
+    g.wait_ge(sem.loaded, 16)
+
+    dests = [world(1 - host, chip, gatherer)]
+    if k != gatherer:
+        dests.append(here(gatherer))
+    g.remote_dma_fused([transfer(staged, mine, dests, 0x00FF, sem.hop1)], local_sem=sem.sent)
+    sent += 8
+
+    if pos == 0:
+        blk = 16 * (k // 4) + chip
+        g.wait_ge(sem.hop1, 8 * (7 if k == gatherer else 8))
+        dests = [world(host, c, collector_of(c, blk)) for c in range(chip % 2, 16, 2) if c != chip]
+        dests.append(here(k + 2))
+        g.remote_dma_fused([transfer(cols(blk), cols(blk), dests, 0x00FF, sem.hop2)], local_sem=sem.sent)
+        sent += 8
+
+    first = 4 * (4 * (k // 4) + (pos + chip // 4) % 4)
+    same = [first + chip % 2, first + 2 + chip % 2]
+    other = [first + 1 - chip % 2, first + 3 - chip % 2]
+
+    if pos >= 2:
+        g.wait_ge(sem.hop2, 8 * 4)
+        pfirst = 4 * (4 * (k // 4) + (pos - 2 + chip // 4) % 4)
+        calls = []
+        for n, blk in enumerate(same + [pfirst + chip % 2, pfirst + 2 + chip % 2]):
+            o = owner_of(chip, blk)
+            dests = [world(host, chip ^ 1, o)]
+            if o != k and blk % 16 != chip:
+                dests.append(here(o))
+            calls.append(transfer(cols(blk), cols(blk), dests, 0x03 << (2 * n), sem.hop3))
+        g.remote_dma_fused(calls, local_sem=sem.sent)
+        sent += 8
+
+    g.wait_ge(sem.hop3, 2 * (2 if pos >= 2 else 3 if pos == 0 else 4))
+    dests = [here(i) for i in range(8) if i != k and (pos >= 2 or i != k + 2)]
+    g.remote_dma_fused([transfer(cols(first, 4), cols(first, 4), dests, 0xFFFF, sem.hop4)], local_sem=sem.sent)
+    sent += 16
+    if pos < 2:
+        g.remote_dma_fused([transfer(cols(b), cols(b), [here(k + 2)], 0x00FF << (8 * n), sem.hop4)
+                            for n, b in enumerate(other)], local_sem=sem.sent)
+        sent += 16
+
+    g.wait_ge(sem.hop4, 16 * 7)
+    g.wait_ge(sem.sent, sent)
+    g.dma_start(T.y[:], land[:]).then_inc(sem.stored, 16)
+    g.wait_ge(sem.stored, 16)

@@ -59,7 +59,8 @@ def rank_program(g, core, T, topo):
     if pos == 0:
         blk = 16 * (k // 4) + chip
         g.wait_ge(sem.hop1, 8 * (7 if k == gatherer else 8))
-        dests = [world(host, c, collector_of(c, blk)) for c in range(chip % 2, 16, 2) if c != chip]
+        plane = [(chip + 2 * i) % 16 for i in range(1, 8)]
+        dests = [world(host, c, collector_of(c, blk)) for c in plane]
         dests.append(here(k + 2))
         g.remote_dma_fused([transfer(cols(blk), cols(blk), dests, 0x00FF, sem.hop2)], local_sem=sem.sent)
         sent += 8
@@ -82,7 +83,8 @@ def rank_program(g, core, T, topo):
         sent += 8
 
     g.wait_ge(sem.hop3, 2 * (2 if pos >= 2 else 3 if pos == 0 else 4))
-    dests = [here(i) for i in range(8) if i != k and (pos >= 2 or i != k + 2)]
+    ring = [(k + i) % 8 for i in range(1, 8)]
+    dests = [here(i) for i in ring if pos >= 2 or i != k + 2]
     g.remote_dma_fused([transfer(cols(first, 4), cols(first, 4), dests, 0xFFFF, sem.hop4)], local_sem=sem.sent)
     sent += 16
     if pos < 2:

@@ -2,97 +2,143 @@ import concourse.bass as bass
 
 BLK = 16
 CHIPBLK = 8 * BLK
-RANGE = 4 * CHIPBLK
+PAIR = 2 * CHIPBLK
+
+GROUPS = [[0, 1, 2], [3, 4], [5, 6], [7], [8]]
 
 SCRATCH = {
     "land": ("sbuf", [128, 256 * BLK], "float32"),
     "xs": ("sbuf", [128, BLK], "float32"),
 }
-SEMAPHORES = ["loaded", "stored", "sent", "hop1", "hop2", "hop3", "hop4"]
+SEMAPHORES = (["loaded", "stored", "sent", "g1"] + ["sw%d" % i for i in range(4)] + ["mt%d" % i for i in range(4)]
+              + ["bc%d" % i for i in range(len(GROUPS))])
 
 
-def owner_of(chip, blk):
-    return 4 * (blk // 16) + ((blk % 16) // 4 - chip // 4) % 4
+def die_of(o):
+    return 0 if o % 2 else 1
 
 
-def collector_of(chip, blk):
-    o = owner_of(chip, blk)
-    return o if o % 4 >= 2 else o + 2
+def slot_of(o):
+    return (o + 1) // 2
+
+
+def collector_of(o):
+    return 4 * die_of(o) + 2 + slot_of(o) % 2
+
+
+def owner_of(o):
+    return 4 * die_of(o) + slot_of(o) % 2
+
+
+def order_of(o):
+    return (o - 1) // 4 if o % 2 else o // 4
+
+
+def group_of(o):
+    j = slot_of(o)
+    return [n for n, js in enumerate(GROUPS) if j in js][0]
+
+
+def ring(k, skip=()):
+    return [(k + i) % 8 for i in range(1, 8) if (k + i) % 8 not in skip]
+
+
+def onchip_copies(o, from_mate):
+    if from_mate:
+        k = owner_of(o)
+        return k, [(ring(k), 0xFF00 if k % 4 == 0 else 0xFFFF)]
+    k = collector_of(o)
+    d = ring(k, skip=(0, 4) if o == 0 else ())
+    return k, [(d[:-2], 0xFF00), (d[-2:], 0x00F0)]
+
+
+def engines(mask):
+    return bin(mask).count("1")
 
 
 def rank_program(g, core, T, topo):
     host, chip, k = topo.host(core), topo.chip(core), core % 8
-    pos = k % 4
+    par, Q = chip % 2, 8 * host + chip // 2
+    pos, die = k % 4, k // 4
     land, sem = T.land, T.sem
-    sent = 0
+    SW = [sem.sw0, sem.sw1, sem.sw2, sem.sw3]
+    MT = [sem.mt0, sem.mt1, sem.mt2, sem.mt3]
+    BC = [sem.bc0, sem.bc1, sem.bc2, sem.bc3, sem.bc4]
+    sent = [0]
 
-    def world(h, c, i):
-        return 128 * h + 8 * c + i
+    def world(q, p, i):
+        q %= 16
+        return 128 * (q // 8) + 8 * (2 * (q % 8) + p) + i
 
     def here(i):
-        return world(host, chip, i)
+        return world(Q, par, i)
 
-    def cols(blk, n=1):
-        return land[:, CHIPBLK * blk:CHIPBLK * (blk + n)]
+    def cols(o, p):
+        b = 2 * ((Q - o) % 16) + p
+        return land[:, CHIPBLK * b:CHIPBLK * (b + 1)]
 
-    def transfer(src, out, dests, mask, remote_sem):
+    def transfer(ap, dests, mask, remote_sem, src=None):
+        sent[0] += engines(mask)
         ids = []
         for d in dests:
             rid, pid = topo.addr(d, core)
             ids.append(bass.DstId(rid=rid, pnc=pid))
         return bass.RemoteDMATransfer(dst_ids=ids, dma_engine_mask=mask, remote_sem=remote_sem,
-                                      srcs=[src], dsts=[out for d in dests])
+                                      srcs=[ap if src is None else src], dsts=[ap for d in dests])
 
-    rank = T.rank_of(core)
-    mine = land[:, BLK * rank:BLK * (rank + 1)]
-    gatherer = 4 * host
-    staged = mine if k == gatherer else T.xs[:]
+    def call(transfers):
+        g.remote_dma_fused(transfers, local_sem=sem.sent)
+
+    mine = land[:, BLK * core:BLK * (core + 1)]
+    staged = mine if pos == 0 else T.xs[:]
     g.dma_start(staged, T.x[:]).then_inc(sem.loaded, 16)
     g.wait_ge(sem.loaded, 16)
 
-    dests = [world(1 - host, chip, gatherer)]
-    if k != gatherer:
-        dests.append(here(gatherer))
-    g.remote_dma_fused([transfer(staged, mine, dests, 0x00FF, sem.hop1)], local_sem=sem.sent)
-    sent += 8
+    first = [4, 0] if die == 0 else [0, 4]
+    call([transfer(mine, [here(i) for i in first if i != k], 0xFFFF, sem.g1, src=staged)])
 
     if pos == 0:
-        blk = 16 * (k // 4) + chip
-        g.wait_ge(sem.hop1, 8 * (7 if k == gatherer else 8))
-        plane = [(chip + 2 * i) % 16 for i in range(1, 8)]
-        dests = [world(host, c, collector_of(c, blk)) for c in plane]
-        dests.append(here(k + 2))
-        g.remote_dma_fused([transfer(cols(blk), cols(blk), dests, 0x00FF, sem.hop2)], local_sem=sem.sent)
-        sent += 8
+        g.wait_ge(sem.g1, 16 * 7)
+        offs = range(1, 16, 2) if die == 0 else range(2, 16, 2)
+        mysw = SW[Q // 4]
+        trs = [transfer(cols(0, par), [world(Q + o, par, collector_of(o)) for o in offs], 0x00FF, mysw)]
+        if die == 1:
+            trs.append(transfer(cols(0, par), [here(collector_of(0))], 0xFF00, mysw))
+        call(trs)
 
-    first = 4 * (4 * (k // 4) + (pos + chip // 4) % 4)
-    same = [first + chip % 2, first + 2 + chip % 2]
-    other = [first + 1 - chip % 2, first + 3 - chip % 2]
+    mine_offs = [o for o in range(16) if (collector_of(o) if pos >= 2 else owner_of(o)) == k]
+    for o in sorted(mine_offs, key=order_of):
+        grp = BC[group_of(o)]
+        if pos >= 2:
+            g.wait_ge(SW[((Q - o) % 16) // 4], 8)
+            ap = cols(o, par)
+            trs = [transfer(ap, [world(Q, 1 - par, owner_of(o))], 0x000F, MT[order_of(o)])]
+            trs += [transfer(ap, [here(i) for i in d], m, grp) for d, m in onchip_copies(o, False)[1]]
+        else:
+            g.wait_ge(MT[order_of(o)], 4)
+            ap = cols(o, 1 - par)
+            trs = [transfer(ap, [here(i) for i in d], m, grp) for d, m in onchip_copies(o, True)[1]]
+        call(trs)
 
-    if pos >= 2:
-        g.wait_ge(sem.hop2, 8 * 4)
-        pfirst = 4 * (4 * (k // 4) + (pos - 2 + chip // 4) % 4)
-        calls = []
-        for n, blk in enumerate(same + [pfirst + chip % 2, pfirst + 2 + chip % 2]):
-            o = owner_of(chip, blk)
-            dests = [world(host, chip ^ 1, o)]
-            if o != k and blk % 16 != chip:
-                dests.append(here(o))
-            calls.append(transfer(cols(blk), cols(blk), dests, 0x03 << (2 * n), sem.hop3))
-        g.remote_dma_fused(calls, local_sem=sem.sent)
-        sent += 8
-
-    g.wait_ge(sem.hop3, 2 * (2 if pos >= 2 else 3 if pos == 0 else 4))
-    ring = [(k + i) % 8 for i in range(1, 8)]
-    dests = [here(i) for i in ring if pos >= 2 or i != k + 2]
-    g.remote_dma_fused([transfer(cols(first, 4), cols(first, 4), dests, 0xFFFF, sem.hop4)], local_sem=sem.sent)
-    sent += 16
-    if pos < 2:
-        g.remote_dma_fused([transfer(cols(b), cols(b), [here(k + 2)], 0x00FF << (8 * n), sem.hop4)
-                            for n, b in enumerate(other)], local_sem=sem.sent)
-        sent += 16
-
-    g.wait_ge(sem.hop4, 16 * 7)
-    g.wait_ge(sem.sent, sent)
-    g.dma_start(T.y[:], land[:]).then_inc(sem.stored, 16)
-    g.wait_ge(sem.stored, 16)
+    stored = 0
+    for n, js in enumerate(GROUPS):
+        offs = [o for o in range(16) if slot_of(o) in js]
+        expect = 0
+        for o in offs:
+            for fm in (False, True):
+                for d, m in onchip_copies(o, fm)[1]:
+                    if k in d:
+                        expect += engines(m)
+        g.wait_ge(BC[n], expect)
+        pairs = sorted((Q - o) % 16 for o in offs)
+        runs = []
+        for q in pairs:
+            if runs and runs[-1][1] == q:
+                runs[-1][1] = q + 1
+            else:
+                runs.append([q, q + 1])
+        for a, b in runs:
+            g.dma_start(T.y[:, PAIR * a:PAIR * b], land[:, PAIR * a:PAIR * b]).then_inc(sem.stored, 16)
+            stored += 16
+    g.wait_ge(sem.sent, sent[0])
+    g.wait_ge(sem.stored, stored)

import concourse.bass as bass

BLK = 16
CHIPBLK = 8 * BLK
PAIR = 2 * CHIPBLK

GROUPS = [[0, 1, 2], [3, 4], [5, 6], [7], [8]]

SCRATCH = {
    "land": ("sbuf", [128, 256 * BLK], "float32"),
    "xs": ("sbuf", [128, BLK], "float32"),
}
SEMAPHORES = (["loaded", "stored", "sent", "g1"] + ["sw%d" % i for i in range(4)] + ["mt%d" % i for i in range(4)]
              + ["bc%d" % i for i in range(len(GROUPS))])


def die_of(o):
    return 0 if o % 2 else 1


def slot_of(o):
    return (o + 1) // 2


def collector_of(o):
    return 4 * die_of(o) + 2 + slot_of(o) % 2


def owner_of(o):
    return 4 * die_of(o) + slot_of(o) % 2


def order_of(o):
    return (o - 1) // 4 if o % 2 else o // 4


def group_of(o):
    j = slot_of(o)
    return [n for n, js in enumerate(GROUPS) if j in js][0]


def ring(k, skip=()):
    return [(k + i) % 8 for i in range(1, 8) if (k + i) % 8 not in skip]


def onchip_copies(o, from_mate):
    if from_mate:
        k = owner_of(o)
        return k, [(ring(k), 0xFF00 if k % 4 == 0 else 0xFFFF)]
    k = collector_of(o)
    d = ring(k, skip=(0, 4) if o == 0 else ())
    return k, [(d[:-2], 0xFF00), (d[-2:], 0x00F0)]


def engines(mask):
    return bin(mask).count("1")


def rank_program(g, core, T, topo):
    host, chip, k = topo.host(core), topo.chip(core), core % 8
    par, Q = chip % 2, 8 * host + chip // 2
    pos, die = k % 4, k // 4
    land, sem = T.land, T.sem
    SW = [sem.sw0, sem.sw1, sem.sw2, sem.sw3]
    MT = [sem.mt0, sem.mt1, sem.mt2, sem.mt3]
    BC = [sem.bc0, sem.bc1, sem.bc2, sem.bc3, sem.bc4]
    sent = [0]

    def world(q, p, i):
        q %= 16
        return 128 * (q // 8) + 8 * (2 * (q % 8) + p) + i

    def here(i):
        return world(Q, par, i)

    def cols(o, p):
        b = 2 * ((Q - o) % 16) + p
        return land[:, CHIPBLK * b:CHIPBLK * (b + 1)]

    def transfer(ap, dests, mask, remote_sem, src=None):
        sent[0] += engines(mask)
        ids = []
        for d in dests:
            rid, pid = topo.addr(d, core)
            ids.append(bass.DstId(rid=rid, pnc=pid))
        return bass.RemoteDMATransfer(dst_ids=ids, dma_engine_mask=mask, remote_sem=remote_sem,
                                      srcs=[ap if src is None else src], dsts=[ap for d in dests])

    def call(transfers):
        g.remote_dma_fused(transfers, local_sem=sem.sent)

    mine = land[:, BLK * core:BLK * (core + 1)]
    staged = mine if pos == 0 else T.xs[:]
    g.dma_start(staged, T.x[:]).then_inc(sem.loaded, 16)
    g.wait_ge(sem.loaded, 16)

    first = [4, 0] if die == 0 else [0, 4]
    call([transfer(mine, [here(i) for i in first if i != k], 0xFFFF, sem.g1, src=staged)])

    if pos == 0:
        g.wait_ge(sem.g1, 16 * 7)
        offs = range(1, 16, 2) if die == 0 else range(2, 16, 2)
        mysw = SW[Q // 4]
        trs = [transfer(cols(0, par), [world(Q + o, par, collector_of(o)) for o in offs], 0x00FF, mysw)]
        if die == 1:
            trs.append(transfer(cols(0, par), [here(collector_of(0))], 0xFF00, mysw))
        call(trs)

    mine_offs = [o for o in range(16) if (collector_of(o) if pos >= 2 else owner_of(o)) == k]
    for o in sorted(mine_offs, key=order_of):
        grp = BC[group_of(o)]
        if pos >= 2:
            g.wait_ge(SW[((Q - o) % 16) // 4], 8)
            ap = cols(o, par)
            trs = [transfer(ap, [world(Q, 1 - par, owner_of(o))], 0x000F, MT[order_of(o)])]
            trs += [transfer(ap, [here(i) for i in d], m, grp) for d, m in onchip_copies(o, False)[1]]
        else:
            g.wait_ge(MT[order_of(o)], 4)
            ap = cols(o, 1 - par)
            trs = [transfer(ap, [here(i) for i in d], m, grp) for d, m in onchip_copies(o, True)[1]]
        call(trs)

    stored = 0
    for n, js in enumerate(GROUPS):
        offs = [o for o in range(16) if slot_of(o) in js]
        expect = 0
        for o in offs:
            for fm in (False, True):
                for d, m in onchip_copies(o, fm)[1]:
                    if k in d:
                        expect += engines(m)
        g.wait_ge(BC[n], expect)
        pairs = sorted((Q - o) % 16 for o in offs)
        runs = []
        for q in pairs:
            if runs and runs[-1][1] == q:
                runs[-1][1] = q + 1
            else:
                runs.append([q, q + 1])
        for a, b in runs:
            g.dma_start(T.y[:, PAIR * a:PAIR * b], land[:, PAIR * a:PAIR * b]).then_inc(sem.stored, 16)
            stored += 16
    g.wait_ge(sem.sent, sent[0])
    g.wait_ge(sem.stored, stored)
